import numpy as np
import ml_dtypes


def mxq(x, axis, fmt="e4m3"):
    dtype, down = {"e4m3": (ml_dtypes.float8_e4m3fn, 7), "e5m2": (ml_dtypes.float8_e5m2, 14)}[fmt]
    v = np.moveaxis(np.asarray(x, np.float32).astype(ml_dtypes.bfloat16).astype(np.float64), axis, -1)
    blocks = v.reshape(v.shape[:-1] + (-1, 32))
    amax = np.abs(blocks).max(-1, keepdims=True)
    byte = np.maximum(np.where(amax > 0, np.frexp(amax)[1] - 1 + 127, 0) - down, 1)
    scale = np.exp2(byte - 127.0)
    codes = (blocks / scale).astype(np.float32).astype(dtype).astype(np.float64)
    return np.moveaxis((codes * scale).reshape(v.shape), -1, axis)


WIDE = False


def mx_kscale(k):
    if not WIDE:
        return np.ones(k)
    levels = np.array([10, -10, 5, -5, 0])
    if k % 512:
        return np.exp2(np.random.permutation(np.resize(levels, k // 32))).repeat(32)
    a = np.empty((k // 512, 16))
    for p in range(k // 512):
        a[p, :8] = np.random.permutation(np.resize(levels, 8))
        for g in range(8):
            far = levels[np.abs(levels - a[p, g]) >= 10]
            a[p, g + 8] = far[np.random.randint(len(far))]
    return np.exp2(a.ravel()).repeat(32)


def f64(x):
    return np.asarray(x).astype(np.float64)


def striped(idx):
    return np.tile(idx.reshape(-1, 16).T, (8, 1)).astype(np.uint16)


def unstriped(offs):
    return offs[:16].T.reshape(-1).astype(np.int64)


def pack_weight(w):
    k, n = w.shape
    w = f64(np.asarray(w, np.float32).astype(ml_dtypes.bfloat16)).reshape(k // 32, 32, n)
    amax = np.abs(w).max(1)
    byte = np.clip(np.where(amax > 0, np.frexp(amax)[1] - 1 + 127 - 7, 1), 1, 254)
    scaled = (w * np.exp2(127.0 - byte)[:, None, :]).reshape(k, n).astype(np.float32)
    words = np.ascontiguousarray(scaled.reshape(k // 512, 128, 4, n).transpose(0, 1, 3, 2)).astype(ml_dtypes.float8_e4m3fn).view(np.uint8)
    return words, np.ascontiguousarray(byte.astype(np.uint8).reshape(k // 512, 16, n))


def unpack_weight(words, scales):
    g, p, n, _ = words.shape
    vals = np.ascontiguousarray(words).view(ml_dtypes.float8_e4m3fn).astype(np.float64) * np.repeat(np.exp2(scales.astype(np.float64) - 127.0), 8, axis=1)[..., None]
    return vals.transpose(0, 1, 3, 2).reshape(g * 512, n)


E2M1 = np.array([0.0, 0.5, 1.0, 1.5, 2.0, 3.0, 4.0, 6.0, -0.0, -0.5, -1.0, -1.5, -2.0, -3.0, -4.0, -6.0])


def pack_fp4(w):
    k, n = w.shape
    w = f64(np.asarray(w, np.float32).astype(ml_dtypes.bfloat16)).reshape(k // 32, 32, n)
    amax = np.abs(w).max(1)
    mant, ex = np.frexp(amax / 6.0)
    byte = np.clip(np.where(amax > 0, np.where(mant > 0.5, ex, ex - 1) + 127, 1), 1, 254)
    scaled = (w * np.exp2(127.0 - byte)[:, None, :]).reshape(k, n).astype(np.float32)
    c = np.ascontiguousarray(scaled.reshape(k // 512, 128, 4, n).transpose(0, 1, 3, 2)).astype(ml_dtypes.float4_e2m1fn).view(np.uint8) & 0xF
    words = (c[..., 0::2] | (c[..., 1::2] << 4)).reshape(k // 512, 128, 2 * n)
    return np.ascontiguousarray(words), np.ascontiguousarray(byte.astype(np.uint8).reshape(k // 512, 16, n))


def unpack_fp4(words, scales):
    g, _, n = scales.shape
    words = np.ascontiguousarray(words).reshape(g, 128, n, 2)
    nib = np.empty((g, 128, n, 4), np.uint8)
    nib[..., 0::2] = words & 0xF
    nib[..., 1::2] = words >> 4
    vals = E2M1[nib] * np.repeat(np.exp2(scales.astype(np.float64) - 127.0), 8, axis=1)[..., None]
    return vals.transpose(0, 1, 3, 2).reshape(g * 512, n)


K, T, H, N = 1024, 512, 512, 256


def setup_inputs():
    n = np.random.standard_normal
    s = mx_kscale(K)[:, None]
    u = mx_kscale(H)
    packed_xT = pack_weight(n((K, T)) * s)
    packed_w2 = pack_fp4(n((H, N)) / np.sqrt(3 * H) / u[:, None])
    packed_w3 = pack_fp4(n((H, N)) / np.sqrt(3 * H) / u[:, None])
    packed_w4 = pack_fp4(n((H, N)) / np.sqrt(3 * H) / u[:, None])
    return {
        "x_words": packed_xT[0],
        "x_scales": packed_xT[1],
        "w1": (n((K, H)) / np.sqrt(K) / s * u).astype(np.float32),
        "w2_words": packed_w2[0],
        "w2_scales": packed_w2[1],
        "w3_words": packed_w3[0],
        "w3_scales": packed_w3[1],
        "w4_words": packed_w4[0],
        "w4_scales": packed_w4[1],
        "pos1": striped(np.random.permutation(T)),
        "pos2": striped(np.random.permutation(T)),
        "pos3": striped(np.random.permutation(T)),
        "pos4": striped(np.random.permutation(T)),
    }


def reference(x_words, x_scales, w1, w2_words, w2_scales, w3_words, w3_scales, w4_words, w4_scales, pos1, pos2, pos3, pos4):
    xq = unpack_weight(x_words, x_scales)
    h = mxq(f64(w1), 0, "e4m3").T @ xq
    g0 = h[:, unstriped(pos1)]
    g1 = h[:, unstriped(pos2)]
    g2 = h[:, unstriped(pos3)]
    g3 = h[:, unstriped(pos4)]
    z1 = (g0 + g1 + g2 + g3) / 4
    z2 = np.maximum(np.maximum(np.maximum(g0, g1), g2), g3)
    z3 = np.minimum(np.minimum(np.minimum(g0, g1), g2), g3)
    return unpack_fp4(w2_words, w2_scales).T @ mxq(z1, 0, "e4m3") + unpack_fp4(w3_words, w3_scales).T @ mxq(z2, 0, "e4m3") + unpack_fp4(w4_words, w4_scales).T @ mxq(z3, 0, "e4m3")

@@ -1,0 +1,223 @@
+from contextlib import ExitStack
+
+import concourse.mybir as mybir
+from concourse.masks import make_identity
+
+K, T, H, N = 1024, 512, 512, 256
+FLOPS = 2 * K * H * T + 3 * 2 * H * N * T
+
+F32 = mybir.dt.float32
+BF16 = mybir.dt.bfloat16
+I32 = mybir.dt.int32
+U32 = mybir.dt.uint32
+U16 = mybir.dt.uint16
+U8 = mybir.dt.uint8
+FP8X4 = mybir.dt.float8_e4m3fn_x4
+FP4X4 = mybir.dt.float4_e2m1fn_x4
+MAX = mybir.AluOpType.max
+MIN = mybir.AluOpType.min
+COPY = mybir.ActivationFunctionType.Copy
+
+P = 128
+PACK = 4
+PASSES = K // (P * PACK)
+LISTS = 4
+STATS = 3
+BLOCK = 128
+CHUNK = 256
+UNITS = ((0, 256), (256, 128), (384, 128))
+
+
+def tile_picked_wpna_none_l_kernel(
+    tc, x_words, x_scales, w1, w2_words, w2_scales, w3_words, w3_scales, w4_words, w4_scales,
+    pos1, pos2, pos3, pos4, out,
+):
+    nc = tc.nc
+    with ExitStack() as ctx:
+        keep = ctx.enter_context(tc.tile_pool(name="keep", bufs=1))
+        psum = ctx.enter_context(tc.psum_pool(name="psum", bufs=1))
+
+        def sb(name, shape, dtype):
+            return keep.tile(shape, dtype, name=name, align_bytes=64)
+
+        def bank(number, name, shape):
+            return psum.tile(shape, F32, name=name, tag="bank%d" % number)
+
+        x_plane = sb("x_plane", [P, PASSES, T], U8)
+        nc.gpsimd.memset(x_plane[:].rearrange("p g c -> p (g c)").bitcast(U32), 0)
+        w1_raw = []
+        for g in range(PASSES):
+            raw = sb("w1_raw%d" % g, [P, PACK, H], F32)
+            nc.sync.dma_start(out=raw[:], in_=w1[512 * g : 512 * (g + 1), :].rearrange("(p j) c -> p j c", j=PACK))
+            w1_raw.append(raw)
+            if g == 0:
+                for q in range(4):
+                    nc.sync.dma_start(
+                        out=x_plane[32 * q : 32 * q + 4, :, :].bitcast(I32),
+                        in_=x_scales[:, 4 * q : 4 * q + 4, :].rearrange("g r c -> r g c").bitcast(I32),
+                    )
+        x_codes = []
+        for g in range(PASSES):
+            codes = sb("x_codes%d" % g, [P, T], U32)
+            nc.sync.dma_start(out=codes[:].bitcast(I32), in_=x_words[g].rearrange("p n t -> p (n t)").bitcast(I32))
+            x_codes.append(codes)
+        lists = []
+        for d, pos in enumerate((pos1, pos2, pos3, pos4)):
+            offsets = keep.tile([P, T // 16], U16, name="offsets%d" % d)
+            nc.sync.dma_start(offsets[:], pos)
+            lists.append(offsets)
+
+        w_plane = sb("w_plane", [P, STATS, N], U8)
+        nc.gpsimd.memset(w_plane[:].rearrange("p s c -> p (s c)").bitcast(U32), 0)
+        w_codes = []
+        for s, (words, scales) in enumerate(((w2_words, w2_scales), (w3_words, w3_scales), (w4_words, w4_scales))):
+            codes = sb("w_codes%d" % s, [P, 2 * N], U8)
+            nc.sync.dma_start(out=codes[:].bitcast(I32), in_=words[0].bitcast(I32))
+            w_codes.append(codes)
+            for q in range(4):
+                nc.sync.dma_start(
+                    out=w_plane[32 * q : 32 * q + 4, s, :].bitcast(I32),
+                    in_=scales[0, 4 * q : 4 * q + 4, :].bitcast(I32),
+                )
+
+        ident = sb("ident", [P, P], F32)
+        make_identity(nc, ident[:])
+
+        w1_codes = {}
+        w1_planes = {}
+        for g in range(PASSES):
+            dealt = w1_raw[g][:].rearrange("p j (m t) -> p m t j", t=PACK)
+            for u in range(2):
+                grouped = sb("w1_grouped%d_%d" % (g, u), [P, 2 * P * PACK], BF16)
+                target = grouped[:].rearrange("p (e m j) -> p m e j", e=2, j=PACK)
+                if u == 0:
+                    nc.vector.tensor_copy(out=target, in_=dealt[:, :, 0:2, :])
+                else:
+                    nc.scalar.copy(out=target, in_=dealt[:, :, 2:4, :])
+                for e in range(2):
+                    t = 2 * u + e
+                    codes = sb("w1_codes%d_%d" % (g, t), [P, P], U32)
+                    plane = sb("w1_plane%d_%d" % (g, t), [P, P], U8)
+                    nc.vector.quantize_mx(
+                        out=codes[:].bitcast(FP8X4), scales=plane[:], in_=grouped[:, 512 * e : 512 * (e + 1)]
+                    )
+                    w1_codes[g, t] = codes
+                    w1_planes[g, t] = plane
+
+        hidden = []
+        for t in range(PACK):
+            window = sb("hidden%d" % t, [P, T], F32)
+            parts = [(0, slice(0, T // 2)), (4, slice(T // 2, T))] if t == 0 else [(t, slice(0, T))]
+            accs = [bank(number, "h_acc%d" % number, [P, cols.stop - cols.start]) for number, cols in parts]
+            for g in range(PASSES):
+                for acc, (number, cols) in zip(accs, parts):
+                    nc.tensor.matmul_mx(
+                        out=acc[:], lhsT=w1_codes[g, t][:].bitcast(FP8X4), lhsT_scale=w1_planes[g, t][:],
+                        rhs=x_codes[g][:, cols].bitcast(FP8X4), rhs_scale=x_plane[:, g, cols],
+                        start=(g == 0), stop=(g == PASSES - 1),
+                    )
+            for acc, (number, cols) in zip(accs, parts):
+                if number == 0:
+                    nc.vector.tensor_copy(out=window[:, cols], in_=acc[:])
+                else:
+                    nc.scalar.copy(out=window[:, cols], in_=acc[:])
+            hidden.append(window)
+
+        rounded = {}
+        means = {}
+
+        def gather(c):
+            v0, n = c * CHUNK, CHUNK
+            picked = [sb("picked%d_%d" % (c, d), [P, PACK, n], F32) for d in range(LISTS)]
+            for t in range(PACK):
+                for d in range(LISTS):
+                    nc.vector.tensor_copy(
+                        out=picked[d][:, t, :], in_=hidden[t][:].indirect(lists[d][:, v0 // 16 : (v0 + n) // 16])
+                    )
+            for d in range(LISTS):
+                woven = sb("rounded%d_%d" % (c, d), [P, n * PACK], BF16)
+                nc.scalar.copy(
+                    out=woven[:].rearrange("p (a i t) -> p a t i", i=4, t=PACK),
+                    in_=picked[d][:].rearrange("p t (a i) -> p a t i", i=4),
+                )
+                rounded[c, d] = woven
+            mean = sb("mean%d" % c, [P, n * PACK], BF16)
+            for b in range(n // BLOCK):
+                vb = v0 // BLOCK + b
+                turned = bank(vb, "turned%d" % vb, [P, PACK * P])
+                for t in range(PACK):
+                    for d in range(LISTS):
+                        nc.tensor.matmul(
+                            out=turned[:, P * t : P * (t + 1)], lhsT=picked[d][:, t, BLOCK * b : BLOCK * (b + 1)],
+                            rhs=ident[:], start=(d == 0), stop=(d == LISTS - 1), is_transpose=True,
+                        )
+                mean_t = sb("mean_t%d" % vb, [P, PACK * P], BF16)
+                nc.scalar.activation(
+                    out=mean_t[:].rearrange("v (u p e) -> v u p e", u=2, e=2),
+                    in_=turned[:].rearrange("v (u e p) -> v u p e", u=2, e=2),
+                    func=COPY, scale=1.0 / LISTS,
+                )
+                pairs = mean_t[:].bitcast(F32)
+                back = bank(4 + vb % 2, "back%d" % vb, [P, 2, BLOCK])
+                for u in range(2):
+                    nc.tensor.transpose(back[:, u, :], pairs[:, P * u : P * (u + 1)], ident[:])
+                nc.scalar.copy(
+                    out=mean[:, PACK * BLOCK * b : PACK * BLOCK * (b + 1)].bitcast(F32).rearrange("p (v u) -> p v u", u=2),
+                    in_=back[:].rearrange("p u v -> p v u"),
+                )
+            means[c] = mean
+
+        def finish(number, v0, n):
+            c = v0 // CHUNK
+            width = n * PACK
+            cols = slice((v0 - c * CHUNK) * PACK, (v0 - c * CHUNK + n) * PACK)
+            last = v0 + n == T
+            codes = [sb("z_codes%d_%d" % (number, s), [P, n], U32) for s in range(STATS)]
+            planes = [sb("z_plane%d_%d" % (number, s), [P, n], U8) for s in range(STATS)]
+            nc.vector.quantize_mx(out=codes[0][:].bitcast(FP8X4), scales=planes[0][:], in_=means[c][:, cols])
+            level = sb("level%d" % number, [P, 4, width], BF16)
+            for half in range(2):
+                for s, op in enumerate((MAX, MIN)):
+                    nc.vector.tensor_tensor(
+                        level[:, 2 * s + half, :], rounded[c, 2 * half][:, cols], rounded[c, 2 * half + 1][:, cols], op
+                    )
+            ends = [sb("ends%d_%d" % (number, s), [P, width], BF16) for s in range(2)]
+            for s, op in enumerate((MAX, MIN)):
+                nc.vector.tensor_tensor(ends[s][:], level[:, 2 * s, :], level[:, 2 * s + 1, :], op)
+            for s in range(2):
+                nc.vector.quantize_mx(out=codes[s + 1][:].bitcast(FP8X4), scales=planes[s + 1][:], in_=ends[s][:])
+
+            def product(target, mt, s, b):
+                nc.tensor.matmul_mx(
+                    out=target,
+                    lhsT=w_codes[s][:, 2 * P * mt : 2 * P * (mt + 1)].bitcast(FP4X4),
+                    lhsT_scale=w_plane[:, s, P * mt : P * (mt + 1)],
+                    rhs=codes[s][:, BLOCK * b : BLOCK * (b + 1)].bitcast(FP8X4),
+                    rhs_scale=planes[s][:, BLOCK * b : BLOCK * (b + 1)],
+                    start=(s == 0), stop=(s == STATS - 1),
+                )
+
+            if last:
+                accs = [bank(mt, "out_last%d" % mt, [P, n]) for mt in range(N // P)]
+                for s in range(STATS):
+                    for mt in range(N // P):
+                        product(accs[mt][:], mt, s, 0)
+                results = [sb("result_last%d" % mt, [P, n], F32) for mt in range(N // P)]
+                nc.vector.tensor_copy(out=results[0][:], in_=accs[0][:])
+                nc.sync.dma_start(out=out[0:P, v0 : v0 + n], in_=results[0][:])
+                nc.scalar.copy(out=results[1][:], in_=accs[1][:])
+                nc.scalar.dma_start(out=out[P : 2 * P, v0 : v0 + n], in_=results[1][:])
+            else:
+                acc = bank(6 + number % 2, "out_acc%d" % number, [P, N // P, n])
+                for b in range(n // BLOCK):
+                    for mt in range(N // P):
+                        for s in range(STATS):
+                            product(acc[:, mt, BLOCK * b : BLOCK * (b + 1)], mt, s, b)
+                result = sb("result%d" % number, [P, N // P, n], F32)
+                nc.scalar.copy(out=result[:], in_=acc[:])
+                nc.sync.dma_start(out=out.rearrange("(mt p) v -> p mt v", p=P)[:, :, v0 : v0 + n], in_=result[:])
+
+        for c in range(T // CHUNK):
+            gather(c)
+        for number, (v0, n) in enumerate(UNITS):
+            finish(number, v0, n)

@@ -24,8 +24,8 @@ PASSES = K // (P * PACK)
 LISTS = 4
 STATS = 3
 BLOCK = 128
-CHUNK = 256
-UNITS = ((0, 256), (256, 128), (384, 128))
+HALF = T // 2
+WINDOW = 704
 
 
 def tile_picked_wpna_none_l_kernel(
@@ -37,8 +37,8 @@ def tile_picked_wpna_none_l_kernel(
         keep = ctx.enter_context(tc.tile_pool(name="keep", bufs=1))
         psum = ctx.enter_context(tc.psum_pool(name="psum", bufs=1))
 
-        def sb(name, shape, dtype):
-            return keep.tile(shape, dtype, name=name, align_bytes=64)
+        def sb(name, shape, dtype, tag=None):
+            return keep.tile(shape, dtype, name=name, tag=tag or name, align_bytes=64)
 
         def bank(number, name, shape):
             return psum.tile(shape, F32, name=name, tag="bank%d" % number)
@@ -106,9 +106,10 @@ def tile_picked_wpna_none_l_kernel(
 
         hidden = []
         for t in range(PACK):
-            window = sb("hidden%d" % t, [P, T], F32)
-            parts = [(0, slice(0, T // 2)), (4, slice(T // 2, T))] if t == 0 else [(t, slice(0, T))]
-            accs = [bank(number, "h_acc%d" % number, [P, cols.stop - cols.start]) for number, cols in parts]
+            window = sb("hidden%d" % t, [P, WINDOW], F32)
+            nc.gpsimd.memset(window[:, T:WINDOW], 0.0)
+            parts = [(0, slice(0, HALF)), (1, slice(HALF, T))] if t == 0 else [(0, slice(0, T))]
+            accs = [bank(number, "h_acc%d_%d" % (t, number), [P, cols.stop - cols.start]) for number, cols in parts]
             for g in range(PASSES):
                 for acc, (number, cols) in zip(accs, parts):
                     nc.tensor.matmul_mx(
@@ -117,107 +118,138 @@ def tile_picked_wpna_none_l_kernel(
                         start=(g == 0), stop=(g == PASSES - 1),
                     )
             for acc, (number, cols) in zip(accs, parts):
-                if number == 0:
+                if t == 0 and number == 0:
                     nc.vector.tensor_copy(out=window[:, cols], in_=acc[:])
                 else:
                     nc.scalar.copy(out=window[:, cols], in_=acc[:])
             hidden.append(window)
 
+        early = [(d, 0, T) for d in range(2)]
+        late = {v0: [(d, v0, HALF) for d in range(2, LISTS)] for v0 in (0, HALF)}
+        picked = {}
         rounded = {}
-        means = {}
+        for piece in early + late[0] + late[HALF]:
+            d, v0, n = piece
+            tag = {(2, 0): "x_codes1", (3, 0): "x_plane", (2, HALF): "w1_codes1_3", (3, HALF): "w1_plane1_3"}.get((d, v0))
+            picked[piece] = sb("picked%d_%d" % (d, v0), [P, PACK, n], F32, tag=tag)
+            rounded[piece] = sb("rounded%d_%d" % (d, v0), [P, n * PACK], BF16)
+        turned = [bank((2, 3, 6, 7)[vb], "turned%d" % vb, [P, PACK * P]) for vb in range(T // BLOCK)]
+        mean = {v0: sb("mean%d" % v0, [P, HALF * PACK], BF16) for v0 in (0, HALF)}
 
-        def gather(c):
-            v0, n = c * CHUNK, CHUNK
-            picked = [sb("picked%d_%d" % (c, d), [P, PACK, n], F32) for d in range(LISTS)]
-            for t in range(PACK):
-                for d in range(LISTS):
-                    nc.vector.tensor_copy(
-                        out=picked[d][:, t, :], in_=hidden[t][:].indirect(lists[d][:, v0 // 16 : (v0 + n) // 16])
+        def gather(t, piece):
+            d, v0, n = piece
+            nc.vector.tensor_copy(
+                out=picked[piece][:, t, :], in_=hidden[t][:].indirect(lists[d][:, v0 // 16 : (v0 + n) // 16])
+            )
+
+        def weave(piece):
+            nc.scalar.copy(
+                out=rounded[piece][:].rearrange("p (a i t) -> p a t i", i=4, t=PACK),
+                in_=picked[piece][:].rearrange("p t (a i) -> p a t i", i=4),
+            )
+
+        def add_up(t, v0):
+            pieces = late[v0] + early
+            for vb in range(v0 // BLOCK, (v0 + HALF) // BLOCK):
+                for piece in pieces:
+                    col = BLOCK * vb - piece[1]
+                    nc.tensor.matmul(
+                        out=turned[vb][:, P * t : P * (t + 1)], lhsT=picked[piece][:, t, col : col + BLOCK],
+                        rhs=ident[:], start=(piece == pieces[0]), stop=(piece == pieces[-1]), is_transpose=True,
                     )
-            for d in range(LISTS):
-                woven = sb("rounded%d_%d" % (c, d), [P, n * PACK], BF16)
-                nc.scalar.copy(
-                    out=woven[:].rearrange("p (a i t) -> p a t i", i=4, t=PACK),
-                    in_=picked[d][:].rearrange("p t (a i) -> p a t i", i=4),
-                )
-                rounded[c, d] = woven
-            mean = sb("mean%d" % c, [P, n * PACK], BF16)
-            for b in range(n // BLOCK):
-                vb = v0 // BLOCK + b
-                turned = bank(vb, "turned%d" % vb, [P, PACK * P])
-                for t in range(PACK):
-                    for d in range(LISTS):
-                        nc.tensor.matmul(
-                            out=turned[:, P * t : P * (t + 1)], lhsT=picked[d][:, t, BLOCK * b : BLOCK * (b + 1)],
-                            rhs=ident[:], start=(d == 0), stop=(d == LISTS - 1), is_transpose=True,
-                        )
+
+        def turn_back(v0):
+            blocks = range(v0 // BLOCK, (v0 + HALF) // BLOCK)
+            backs = {}
+            for vb in blocks:
                 mean_t = sb("mean_t%d" % vb, [P, PACK * P], BF16)
                 nc.scalar.activation(
                     out=mean_t[:].rearrange("v (u p e) -> v u p e", u=2, e=2),
-                    in_=turned[:].rearrange("v (u e p) -> v u p e", u=2, e=2),
+                    in_=turned[vb][:].rearrange("v (u e p) -> v u p e", u=2, e=2),
                     func=COPY, scale=1.0 / LISTS,
                 )
                 pairs = mean_t[:].bitcast(F32)
-                back = bank(4 + vb % 2, "back%d" % vb, [P, 2, BLOCK])
+                backs[vb] = bank(4 + vb % 2, "back%d" % vb, [P, 2, BLOCK])
                 for u in range(2):
-                    nc.tensor.transpose(back[:, u, :], pairs[:, P * u : P * (u + 1)], ident[:])
+                    nc.tensor.transpose(backs[vb][:, u, :], pairs[:, P * u : P * (u + 1)], ident[:])
+            for vb in blocks:
+                col = PACK * (BLOCK * vb - v0)
                 nc.scalar.copy(
-                    out=mean[:, PACK * BLOCK * b : PACK * BLOCK * (b + 1)].bitcast(F32).rearrange("p (v u) -> p v u", u=2),
-                    in_=back[:].rearrange("p u v -> p v u"),
+                    out=mean[v0][:, col : col + PACK * BLOCK].bitcast(F32).rearrange("p (v u) -> p v u", u=2),
+                    in_=backs[vb][:].rearrange("p u v -> p v u"),
                 )
-            means[c] = mean
 
-        def finish(number, v0, n):
-            c = v0 // CHUNK
+        for t in range(PACK):
+            for piece in early:
+                gather(t, piece)
+        for piece in early:
+            weave(piece)
+        for v0 in (0, HALF):
+            for t in range(PACK):
+                for piece in late[v0]:
+                    gather(t, piece)
+                add_up(t, v0)
+            for piece in late[v0]:
+                weave(piece)
+            turn_back(v0)
+
+        first = [sb("first%d" % s, [P, T * PACK], BF16) for s in range(2)]
+        second = [sb("second%d" % s, [P, T * PACK], BF16) for s in range(2)]
+        for s, op in enumerate((MAX, MIN)):
+            nc.vector.tensor_tensor(first[s][:], rounded[early[0]][:], rounded[early[1]][:], op)
+
+        def quantise(name, values, n):
+            codes = sb(name + "_codes", [P, n], U32)
+            plane = sb(name + "_plane", [P, n], U8)
+            nc.vector.quantize_mx(out=codes[:].bitcast(FP8X4), scales=plane[:], in_=values)
+            return codes, plane
+
+        def product(target, mt, s, order, moving, col):
+            codes, plane = moving
+            nc.tensor.matmul_mx(
+                out=target,
+                lhsT=w_codes[s][:, 2 * P * mt : 2 * P * (mt + 1)].bitcast(FP4X4),
+                lhsT_scale=w_plane[:, s, P * mt : P * (mt + 1)],
+                rhs=codes[:, col : col + BLOCK].bitcast(FP8X4),
+                rhs_scale=plane[:, col : col + BLOCK],
+                start=(s == order[0]), stop=(s == order[-1]),
+            )
+
+        means = {}
+
+        def finish(number, v0, n, mean_col):
             width = n * PACK
-            cols = slice((v0 - c * CHUNK) * PACK, (v0 - c * CHUNK + n) * PACK)
-            last = v0 + n == T
-            codes = [sb("z_codes%d_%d" % (number, s), [P, n], U32) for s in range(STATS)]
-            planes = [sb("z_plane%d_%d" % (number, s), [P, n], U8) for s in range(STATS)]
-            nc.vector.quantize_mx(out=codes[0][:].bitcast(FP8X4), scales=planes[0][:], in_=means[c][:, cols])
-            level = sb("level%d" % number, [P, 4, width], BF16)
-            for half in range(2):
-                for s, op in enumerate((MAX, MIN)):
-                    nc.vector.tensor_tensor(
-                        level[:, 2 * s + half, :], rounded[c, 2 * half][:, cols], rounded[c, 2 * half + 1][:, cols], op
-                    )
-            ends = [sb("ends%d_%d" % (number, s), [P, width], BF16) for s in range(2)]
+            cols = slice(v0 * PACK, (v0 + n) * PACK)
+            ends = sb("ends%d" % number, [P, 2 * width], BF16)
             for s, op in enumerate((MAX, MIN)):
-                nc.vector.tensor_tensor(ends[s][:], level[:, 2 * s, :], level[:, 2 * s + 1, :], op)
-            for s in range(2):
-                nc.vector.quantize_mx(out=codes[s + 1][:].bitcast(FP8X4), scales=planes[s + 1][:], in_=ends[s][:])
-
-            def product(target, mt, s, b):
-                nc.tensor.matmul_mx(
-                    out=target,
-                    lhsT=w_codes[s][:, 2 * P * mt : 2 * P * (mt + 1)].bitcast(FP4X4),
-                    lhsT_scale=w_plane[:, s, P * mt : P * (mt + 1)],
-                    rhs=codes[s][:, BLOCK * b : BLOCK * (b + 1)].bitcast(FP8X4),
-                    rhs_scale=planes[s][:, BLOCK * b : BLOCK * (b + 1)],
-                    start=(s == 0), stop=(s == STATS - 1),
-                )
-
-            if last:
-                accs = [bank(mt, "out_last%d" % mt, [P, n]) for mt in range(N // P)]
+                nc.vector.tensor_tensor(ends[:, s * width : (s + 1) * width], first[s][:, cols], second[s][:, cols], op)
+            both = [quantise("ends%d_%d" % (number, s), ends[:, s * width : (s + 1) * width], n) for s in range(2)]
+            if v0 + n == T:
+                moving = [(means[v0 - mean_col], mean_col), (both[0], 0), (both[1], 0)]
+                accs = [bank(2 + mt, "out_last%d" % mt, [P, n]) for mt in range(N // P)]
                 for s in range(STATS):
                     for mt in range(N // P):
-                        product(accs[mt][:], mt, s, 0)
+                        product(accs[mt][:], mt, s, (0, 1, 2), *moving[s])
                 results = [sb("result_last%d" % mt, [P, n], F32) for mt in range(N // P)]
                 nc.vector.tensor_copy(out=results[0][:], in_=accs[0][:])
                 nc.sync.dma_start(out=out[0:P, v0 : v0 + n], in_=results[0][:])
                 nc.scalar.copy(out=results[1][:], in_=accs[1][:])
                 nc.scalar.dma_start(out=out[P : 2 * P, v0 : v0 + n], in_=results[1][:])
             else:
-                acc = bank(6 + number % 2, "out_acc%d" % number, [P, N // P, n])
+                means[v0] = quantise("mean%d" % v0, mean[v0][:], HALF)
+                acc = bank(4 + number % 2, "out_acc%d" % number, [P, N // P, n])
                 for b in range(n // BLOCK):
+                    moving = [(means[v0], BLOCK * b), (both[0], BLOCK * b), (both[1], BLOCK * b)]
                     for mt in range(N // P):
-                        for s in range(STATS):
-                            product(acc[:, mt, BLOCK * b : BLOCK * (b + 1)], mt, s, b)
+                        for s in (1, 2, 0):
+                            product(acc[:, mt, BLOCK * b : BLOCK * (b + 1)], mt, s, (1, 2, 0), *moving[s])
                 result = sb("result%d" % number, [P, N // P, n], F32)
                 nc.scalar.copy(out=result[:], in_=acc[:])
                 nc.sync.dma_start(out=out.rearrange("(mt p) v -> p mt v", p=P)[:, :, v0 : v0 + n], in_=result[:])
 
-        for c in range(T // CHUNK):
-            gather(c)
-        for number, (v0, n) in enumerate(UNITS):
-            finish(number, v0, n)
+        for half, units in enumerate((((0, HALF),), ((HALF, BLOCK), (HALF + BLOCK, BLOCK)))):
+            cols = slice(half * HALF * PACK, (half + 1) * HALF * PACK)
+            for s, op in enumerate((MAX, MIN)):
+                nc.vector.tensor_tensor(second[s][:, cols], rounded[late[half * HALF][0]][:], rounded[late[half * HALF][1]][:], op)
+            for k, (v0, n) in enumerate(units):
+                finish(half + k, v0, n, v0 - half * HALF)

@@ -44,7 +44,7 @@ def tile_picked_wpna_none_l_kernel(
             return psum.tile(shape, F32, name=name, tag="bank%d" % number)
 
         x_plane = sb("x_plane", [P, PASSES, T], U8)
-        nc.gpsimd.memset(x_plane[:].rearrange("p g c -> p (g c)").bitcast(U32), 0)
+        nc.vector.memset(x_plane[:].rearrange("p g c -> p (g c)").bitcast(U32), 0)
         w1_raw = []
         for g in range(PASSES):
             raw = sb("w1_raw%d" % g, [P, PACK, H], F32)
@@ -59,7 +59,9 @@ def tile_picked_wpna_none_l_kernel(
         x_codes = []
         for g in range(PASSES):
             codes = sb("x_codes%d" % g, [P, T], U32)
-            nc.sync.dma_start(out=codes[:].bitcast(I32), in_=x_words[g].rearrange("p n t -> p (n t)").bitcast(I32))
+            words = x_words[g].rearrange("p n t -> p (n t)").bitcast(I32)
+            for cols in [slice(0, T)] if g == 0 else [slice(0, HALF), slice(HALF, T)]:
+                nc.sync.dma_start(out=codes[:, cols].bitcast(I32), in_=words[:, cols])
             x_codes.append(codes)
         lists = []
         for d, pos in enumerate((pos1, pos2, pos3, pos4)):
@@ -68,7 +70,7 @@ def tile_picked_wpna_none_l_kernel(
             lists.append(offsets)
 
         w_plane = sb("w_plane", [P, STATS, N], U8)
-        nc.gpsimd.memset(w_plane[:].rearrange("p s c -> p (s c)").bitcast(U32), 0)
+        nc.vector.memset(w_plane[:].rearrange("p s c -> p (s c)").bitcast(U32), 0)
         w_codes = []
         for s, (words, scales) in enumerate(((w2_words, w2_scales), (w3_words, w3_scales), (w4_words, w4_scales))):
             codes = sb("w_codes%d" % s, [P, 2 * N], U8)
@@ -107,8 +109,8 @@ def tile_picked_wpna_none_l_kernel(
         hidden = []
         for t in range(PACK):
             window = sb("hidden%d" % t, [P, WINDOW], F32)
-            nc.gpsimd.memset(window[:, T:WINDOW], 0.0)
-            parts = [(0, slice(0, HALF)), (1, slice(HALF, T))] if t == 0 else [(0, slice(0, T))]
+            nc.vector.memset(window[:, T:WINDOW], 0.0)
+            parts = [(0, slice(0, HALF)), (1, slice(HALF, T))] if t == 0 else [((t + 1) % 2, slice(0, T))]
             accs = [bank(number, "h_acc%d_%d" % (t, number), [P, cols.stop - cols.start]) for number, cols in parts]
             for g in range(PASSES):
                 for acc, (number, cols) in zip(accs, parts):
@@ -133,7 +135,7 @@ def tile_picked_wpna_none_l_kernel(
             tag = {(2, 0): "x_codes1", (3, 0): "x_plane", (2, HALF): "w1_codes1_3", (3, HALF): "w1_plane1_3"}.get((d, v0))
             picked[piece] = sb("picked%d_%d" % (d, v0), [P, PACK, n], F32, tag=tag)
             rounded[piece] = sb("rounded%d_%d" % (d, v0), [P, n * PACK], BF16)
-        turned = [bank((2, 3, 6, 7)[vb], "turned%d" % vb, [P, PACK * P]) for vb in range(T // BLOCK)]
+        turned = {}
         mean = {v0: sb("mean%d" % v0, [P, HALF * PACK], BF16) for v0 in (0, HALF)}
 
         def gather(t, piece):
@@ -158,10 +160,10 @@ def tile_picked_wpna_none_l_kernel(
                         rhs=ident[:], start=(piece == pieces[0]), stop=(piece == pieces[-1]), is_transpose=True,
                     )
 
+        backs = {}
+
         def turn_back(v0):
-            blocks = range(v0 // BLOCK, (v0 + HALF) // BLOCK)
-            backs = {}
-            for vb in blocks:
+            for vb in range(v0 // BLOCK, (v0 + HALF) // BLOCK):
                 mean_t = sb("mean_t%d" % vb, [P, PACK * P], BF16)
                 nc.scalar.activation(
                     out=mean_t[:].rearrange("v (u p e) -> v u p e", u=2, e=2),
@@ -172,7 +174,9 @@ def tile_picked_wpna_none_l_kernel(
                 backs[vb] = bank(4 + vb % 2, "back%d" % vb, [P, 2, BLOCK])
                 for u in range(2):
                     nc.tensor.transpose(backs[vb][:, u, :], pairs[:, P * u : P * (u + 1)], ident[:])
-            for vb in blocks:
+
+        def land(v0):
+            for vb in range(v0 // BLOCK, (v0 + HALF) // BLOCK):
                 col = PACK * (BLOCK * vb - v0)
                 nc.scalar.copy(
                     out=mean[v0][:, col : col + PACK * BLOCK].bitcast(F32).rearrange("p (v u) -> p v u", u=2),
@@ -185,16 +189,22 @@ def tile_picked_wpna_none_l_kernel(
         for piece in early:
             weave(piece)
         for v0 in (0, HALF):
+            for vb in range(v0 // BLOCK, (v0 + HALF) // BLOCK):
+                turned[vb] = bank(2 + vb % 2, "turned%d" % vb, [P, PACK * P])
             for t in range(PACK):
                 for piece in late[v0]:
                     gather(t, piece)
                 add_up(t, v0)
-            for piece in late[v0]:
-                weave(piece)
-            turn_back(v0)
+            if v0 == 0:
+                turn_back(v0)
+                land(v0)
+            weave(late[v0][0])
+            if v0 > 0:
+                turn_back(v0)
+            weave(late[v0][1])
+        land(HALF)
 
         first = [sb("first%d" % s, [P, T * PACK], BF16) for s in range(2)]
-        second = [sb("second%d" % s, [P, T * PACK], BF16) for s in range(2)]
         for s, op in enumerate((MAX, MIN)):
             nc.vector.tensor_tensor(first[s][:], rounded[early[0]][:], rounded[early[1]][:], op)
 
@@ -204,7 +214,22 @@ def tile_picked_wpna_none_l_kernel(
             nc.vector.quantize_mx(out=codes[:].bitcast(FP8X4), scales=plane[:], in_=values)
             return codes, plane
 
-        def product(target, mt, s, order, moving, col):
+        def pair_up(v0):
+            second = [sb("second%d_%d" % (v0, s), [P, HALF * PACK], BF16) for s in range(2)]
+            for s, op in enumerate((MAX, MIN)):
+                nc.vector.tensor_tensor(second[s][:], rounded[late[v0][0]][:], rounded[late[v0][1]][:], op)
+            return second
+
+        def extremes(second, half_start, v0, n):
+            ends = [sb("ends%d_%d" % (v0, s), [P, n * PACK], BF16, tag="ends%d_%d" % (half_start, s)) for s in range(2)]
+            col = (v0 - half_start) * PACK
+            for s, op in enumerate((MAX, MIN)):
+                nc.vector.tensor_tensor(
+                    ends[s][:], first[s][:, v0 * PACK : (v0 + n) * PACK], second[s][:, col : col + n * PACK], op
+                )
+            return ends
+
+        def product(target, mt, s, moving, col):
             codes, plane = moving
             nc.tensor.matmul_mx(
                 out=target,
@@ -212,44 +237,40 @@ def tile_picked_wpna_none_l_kernel(
                 lhsT_scale=w_plane[:, s, P * mt : P * (mt + 1)],
                 rhs=codes[:, col : col + BLOCK].bitcast(FP8X4),
                 rhs_scale=plane[:, col : col + BLOCK],
-                start=(s == order[0]), stop=(s == order[-1]),
+                start=(s == 0), stop=(s == STATS - 1),
             )
 
-        means = {}
+        out_tiles = out.rearrange("(mt p) v -> p mt v", p=P)
 
-        def finish(number, v0, n, mean_col):
-            width = n * PACK
-            cols = slice(v0 * PACK, (v0 + n) * PACK)
-            ends = sb("ends%d" % number, [P, 2 * width], BF16)
-            for s, op in enumerate((MAX, MIN)):
-                nc.vector.tensor_tensor(ends[:, s * width : (s + 1) * width], first[s][:, cols], second[s][:, cols], op)
-            both = [quantise("ends%d_%d" % (number, s), ends[:, s * width : (s + 1) * width], n) for s in range(2)]
-            if v0 + n == T:
-                moving = [(means[v0 - mean_col], mean_col), (both[0], 0), (both[1], 0)]
-                accs = [bank(2 + mt, "out_last%d" % mt, [P, n]) for mt in range(N // P)]
+        moving = [quantise("mean0", mean[0][:], HALF)]
+        ends = extremes(pair_up(0), 0, 0, HALF)
+        moving.extend(quantise("ends0_%d" % s, ends[s][:], HALF) for s in range(2))
+        acc = bank(4, "out_acc", [P, N // P, HALF])
+        for b in range(HALF // BLOCK):
+            for mt in range(N // P):
                 for s in range(STATS):
-                    for mt in range(N // P):
-                        product(accs[mt][:], mt, s, (0, 1, 2), *moving[s])
-                results = [sb("result_last%d" % mt, [P, n], F32) for mt in range(N // P)]
-                nc.vector.tensor_copy(out=results[0][:], in_=accs[0][:])
-                nc.sync.dma_start(out=out[0:P, v0 : v0 + n], in_=results[0][:])
-                nc.scalar.copy(out=results[1][:], in_=accs[1][:])
-                nc.scalar.dma_start(out=out[P : 2 * P, v0 : v0 + n], in_=results[1][:])
-            else:
-                means[v0] = quantise("mean%d" % v0, mean[v0][:], HALF)
-                acc = bank(4 + number % 2, "out_acc%d" % number, [P, N // P, n])
-                for b in range(n // BLOCK):
-                    moving = [(means[v0], BLOCK * b), (both[0], BLOCK * b), (both[1], BLOCK * b)]
-                    for mt in range(N // P):
-                        for s in (1, 2, 0):
-                            product(acc[:, mt, BLOCK * b : BLOCK * (b + 1)], mt, s, (1, 2, 0), *moving[s])
-                result = sb("result%d" % number, [P, N // P, n], F32)
-                nc.scalar.copy(out=result[:], in_=acc[:])
-                nc.sync.dma_start(out=out.rearrange("(mt p) v -> p mt v", p=P)[:, :, v0 : v0 + n], in_=result[:])
+                    product(acc[:, mt, BLOCK * b : BLOCK * (b + 1)], mt, s, moving[s], BLOCK * b)
+        result = sb("result0", [P, N // P, HALF], F32)
+        nc.scalar.copy(out=result[:], in_=acc[:])
+        nc.sync.dma_start(out=out_tiles[:, :, 0:HALF], in_=result[:])
 
-        for half, units in enumerate((((0, HALF),), ((HALF, BLOCK), (HALF + BLOCK, BLOCK)))):
-            cols = slice(half * HALF * PACK, (half + 1) * HALF * PACK)
-            for s, op in enumerate((MAX, MIN)):
-                nc.vector.tensor_tensor(second[s][:, cols], rounded[late[half * HALF][0]][:], rounded[late[half * HALF][1]][:], op)
-            for k, (v0, n) in enumerate(units):
-                finish(half + k, v0, n, v0 - half * HALF)
+        second = pair_up(HALF)
+        for v0 in (HALF, HALF + BLOCK):
+            last = v0 + BLOCK == T
+            ends = extremes(second, HALF, v0, BLOCK)
+            if not last:
+                means = quantise("mean%d" % HALF, mean[HALF][:], HALF)
+            moving = [(means, v0 - HALF)]
+            moving.extend((quantise("ends%d_%d" % (v0, s), ends[s][:], BLOCK), 0) for s in range(2))
+            accs = [bank((0 if last else 6) + mt, "out_acc%d_%d" % (v0, mt), [P, BLOCK]) for mt in range(N // P)]
+            for s in range(STATS):
+                for mt in range(N // P):
+                    product(accs[mt][:], mt, s, *moving[s])
+            for mt in range(N // P):
+                result = sb("result%d_%d" % (v0, mt), [P, BLOCK], F32)
+                if last and mt == 0:
+                    nc.vector.tensor_copy(out=result[:], in_=accs[mt][:])
+                else:
+                    nc.scalar.copy(out=result[:], in_=accs[mt][:])
+                queue = nc.scalar if last and mt == 1 else nc.sync
+                queue.dma_start(out=out_tiles[:, mt, v0 : v0 + BLOCK], in_=result[:])

@@ -120,10 +120,7 @@ def tile_picked_wpna_none_l_kernel(
                         start=(g == 0), stop=(g == PASSES - 1),
                     )
             for acc, (number, cols) in zip(accs, parts):
-                if t == 0 and number == 0:
-                    nc.vector.tensor_copy(out=window[:, cols], in_=acc[:])
-                else:
-                    nc.scalar.copy(out=window[:, cols], in_=acc[:])
+                nc.scalar.copy(out=window[:, cols], in_=acc[:])
             hidden.append(window)
 
         early = [(d, 0, T) for d in range(2)]

from contextlib import ExitStack

import concourse.mybir as mybir
from concourse.masks import make_identity

K, T, H, N = 1024, 512, 512, 256
FLOPS = 2 * K * H * T + 3 * 2 * H * N * T

F32 = mybir.dt.float32
BF16 = mybir.dt.bfloat16
I32 = mybir.dt.int32
U32 = mybir.dt.uint32
U16 = mybir.dt.uint16
U8 = mybir.dt.uint8
FP8X4 = mybir.dt.float8_e4m3fn_x4
FP4X4 = mybir.dt.float4_e2m1fn_x4
MAX = mybir.AluOpType.max
MIN = mybir.AluOpType.min
COPY = mybir.ActivationFunctionType.Copy

P = 128
PACK = 4
PASSES = K // (P * PACK)
LISTS = 4
STATS = 3
BLOCK = 128
HALF = T // 2
WINDOW = 704


def tile_picked_wpna_none_l_kernel(
    tc, x_words, x_scales, w1, w2_words, w2_scales, w3_words, w3_scales, w4_words, w4_scales,
    pos1, pos2, pos3, pos4, out,
):
    nc = tc.nc
    with ExitStack() as ctx:
        keep = ctx.enter_context(tc.tile_pool(name="keep", bufs=1))
        psum = ctx.enter_context(tc.psum_pool(name="psum", bufs=1))

        def sb(name, shape, dtype, tag=None):
            return keep.tile(shape, dtype, name=name, tag=tag or name, align_bytes=64)

        def bank(number, name, shape):
            return psum.tile(shape, F32, name=name, tag="bank%d" % number)

        x_plane = sb("x_plane", [P, PASSES, T], U8)
        nc.vector.memset(x_plane[:].rearrange("p g c -> p (g c)").bitcast(U32), 0)
        w1_raw = []
        for g in range(PASSES):
            raw = sb("w1_raw%d" % g, [P, PACK, H], F32)
            nc.sync.dma_start(out=raw[:], in_=w1[512 * g : 512 * (g + 1), :].rearrange("(p j) c -> p j c", j=PACK))
            w1_raw.append(raw)
            if g == 0:
                for q in range(4):
                    nc.sync.dma_start(
                        out=x_plane[32 * q : 32 * q + 4, :, :].bitcast(I32),
                        in_=x_scales[:, 4 * q : 4 * q + 4, :].rearrange("g r c -> r g c").bitcast(I32),
                    )
        x_codes = []
        for g in range(PASSES):
            codes = sb("x_codes%d" % g, [P, T], U32)
            words = x_words[g].rearrange("p n t -> p (n t)").bitcast(I32)
            for cols in [slice(0, T)] if g == 0 else [slice(0, HALF), slice(HALF, T)]:
                nc.sync.dma_start(out=codes[:, cols].bitcast(I32), in_=words[:, cols])
            x_codes.append(codes)
        lists = []
        for d, pos in enumerate((pos1, pos2, pos3, pos4)):
            offsets = keep.tile([P, T // 16], U16, name="offsets%d" % d)
            nc.sync.dma_start(offsets[:], pos)
            lists.append(offsets)

        w_plane = sb("w_plane", [P, STATS, N], U8)
        nc.vector.memset(w_plane[:].rearrange("p s c -> p (s c)").bitcast(U32), 0)
        w_codes = []
        for s, (words, scales) in enumerate(((w2_words, w2_scales), (w3_words, w3_scales), (w4_words, w4_scales))):
            codes = sb("w_codes%d" % s, [P, 2 * N], U8)
            nc.sync.dma_start(out=codes[:].bitcast(I32), in_=words[0].bitcast(I32))
            w_codes.append(codes)
            for q in range(4):
                nc.sync.dma_start(
                    out=w_plane[32 * q : 32 * q + 4, s, :].bitcast(I32),
                    in_=scales[0, 4 * q : 4 * q + 4, :].bitcast(I32),
                )

        ident = sb("ident", [P, P], F32)
        make_identity(nc, ident[:])

        w1_codes = {}
        w1_planes = {}
        for g in range(PASSES):
            dealt = w1_raw[g][:].rearrange("p j (m t) -> p m t j", t=PACK)
            for u in range(2):
                grouped = sb("w1_grouped%d_%d" % (g, u), [P, 2 * P * PACK], BF16)
                target = grouped[:].rearrange("p (e m j) -> p m e j", e=2, j=PACK)
                if u == 0:
                    nc.vector.tensor_copy(out=target, in_=dealt[:, :, 0:2, :])
                else:
                    nc.scalar.copy(out=target, in_=dealt[:, :, 2:4, :])
                for e in range(2):
                    t = 2 * u + e
                    codes = sb("w1_codes%d_%d" % (g, t), [P, P], U32)
                    plane = sb("w1_plane%d_%d" % (g, t), [P, P], U8)
                    nc.vector.quantize_mx(
                        out=codes[:].bitcast(FP8X4), scales=plane[:], in_=grouped[:, 512 * e : 512 * (e + 1)]
                    )
                    w1_codes[g, t] = codes
                    w1_planes[g, t] = plane

        hidden = []
        for t in range(PACK):
            window = sb("hidden%d" % t, [P, WINDOW], F32)
            nc.vector.memset(window[:, T:WINDOW], 0.0)
            parts = [(0, slice(0, HALF)), (1, slice(HALF, T))] if t == 0 else [((t + 1) % 2, slice(0, T))]
            accs = [bank(number, "h_acc%d_%d" % (t, number), [P, cols.stop - cols.start]) for number, cols in parts]
            for g in range(PASSES):
                for acc, (number, cols) in zip(accs, parts):
                    nc.tensor.matmul_mx(
                        out=acc[:], lhsT=w1_codes[g, t][:].bitcast(FP8X4), lhsT_scale=w1_planes[g, t][:],
                        rhs=x_codes[g][:, cols].bitcast(FP8X4), rhs_scale=x_plane[:, g, cols],
                        start=(g == 0), stop=(g == PASSES - 1),
                    )
            for acc, (number, cols) in zip(accs, parts):
                nc.scalar.copy(out=window[:, cols], in_=acc[:])
            hidden.append(window)

        early = [(d, 0, T) for d in range(2)]
        late = {v0: [(d, v0, HALF) for d in range(2, LISTS)] for v0 in (0, HALF)}
        picked = {}
        rounded = {}
        for piece in early + late[0] + late[HALF]:
            d, v0, n = piece
            tag = {(2, 0): "x_codes1", (3, 0): "x_plane", (2, HALF): "w1_codes1_3", (3, HALF): "w1_plane1_3"}.get((d, v0))
            picked[piece] = sb("picked%d_%d" % (d, v0), [P, PACK, n], F32, tag=tag)
            rounded[piece] = sb("rounded%d_%d" % (d, v0), [P, n * PACK], BF16)
        turned = {}
        mean = {v0: sb("mean%d" % v0, [P, HALF * PACK], BF16) for v0 in (0, HALF)}

        def gather(t, piece):
            d, v0, n = piece
            nc.vector.tensor_copy(
                out=picked[piece][:, t, :], in_=hidden[t][:].indirect(lists[d][:, v0 // 16 : (v0 + n) // 16])
            )

        def weave(piece):
            nc.scalar.copy(
                out=rounded[piece][:].rearrange("p (a i t) -> p a t i", i=4, t=PACK),
                in_=picked[piece][:].rearrange("p t (a i) -> p a t i", i=4),
            )

        def add_up(t, v0):
            pieces = late[v0] + early
            for vb in range(v0 // BLOCK, (v0 + HALF) // BLOCK):
                for piece in pieces:
                    col = BLOCK * vb - piece[1]
                    nc.tensor.matmul(
                        out=turned[vb][:, P * t : P * (t + 1)], lhsT=picked[piece][:, t, col : col + BLOCK],
                        rhs=ident[:], start=(piece == pieces[0]), stop=(piece == pieces[-1]), is_transpose=True,
                    )

        backs = {}

        def turn_back(v0):
            for vb in range(v0 // BLOCK, (v0 + HALF) // BLOCK):
                mean_t = sb("mean_t%d" % vb, [P, PACK * P], BF16)
                nc.scalar.activation(
                    out=mean_t[:].rearrange("v (u p e) -> v u p e", u=2, e=2),
                    in_=turned[vb][:].rearrange("v (u e p) -> v u p e", u=2, e=2),
                    func=COPY, scale=1.0 / LISTS,
                )
                pairs = mean_t[:].bitcast(F32)
                backs[vb] = bank(4 + vb % 2, "back%d" % vb, [P, 2, BLOCK])
                for u in range(2):
                    nc.tensor.transpose(backs[vb][:, u, :], pairs[:, P * u : P * (u + 1)], ident[:])

        def land(v0):
            for vb in range(v0 // BLOCK, (v0 + HALF) // BLOCK):
                col = PACK * (BLOCK * vb - v0)
                nc.scalar.copy(
                    out=mean[v0][:, col : col + PACK * BLOCK].bitcast(F32).rearrange("p (v u) -> p v u", u=2),
                    in_=backs[vb][:].rearrange("p u v -> p v u"),
                )

        for t in range(PACK):
            for piece in early:
                gather(t, piece)
        for piece in early:
            weave(piece)
        for v0 in (0, HALF):
            for vb in range(v0 // BLOCK, (v0 + HALF) // BLOCK):
                turned[vb] = bank(2 + vb % 2, "turned%d" % vb, [P, PACK * P])
            for t in range(PACK):
                for piece in late[v0]:
                    gather(t, piece)
                add_up(t, v0)
            if v0 == 0:
                turn_back(v0)
                land(v0)
            weave(late[v0][0])
            if v0 > 0:
                turn_back(v0)
            weave(late[v0][1])
        land(HALF)

        first = [sb("first%d" % s, [P, T * PACK], BF16) for s in range(2)]
        for s, op in enumerate((MAX, MIN)):
            nc.vector.tensor_tensor(first[s][:], rounded[early[0]][:], rounded[early[1]][:], op)

        def quantise(name, values, n):
            codes = sb(name + "_codes", [P, n], U32)
            plane = sb(name + "_plane", [P, n], U8)
            nc.vector.quantize_mx(out=codes[:].bitcast(FP8X4), scales=plane[:], in_=values)
            return codes, plane

        def pair_up(v0):
            second = [sb("second%d_%d" % (v0, s), [P, HALF * PACK], BF16) for s in range(2)]
            for s, op in enumerate((MAX, MIN)):
                nc.vector.tensor_tensor(second[s][:], rounded[late[v0][0]][:], rounded[late[v0][1]][:], op)
            return second

        def extremes(second, half_start, v0, n):
            ends = [sb("ends%d_%d" % (v0, s), [P, n * PACK], BF16, tag="ends%d_%d" % (half_start, s)) for s in range(2)]
            col = (v0 - half_start) * PACK
            for s, op in enumerate((MAX, MIN)):
                nc.vector.tensor_tensor(
                    ends[s][:], first[s][:, v0 * PACK : (v0 + n) * PACK], second[s][:, col : col + n * PACK], op
                )
            return ends

        def product(target, mt, s, moving, col):
            codes, plane = moving
            nc.tensor.matmul_mx(
                out=target,
                lhsT=w_codes[s][:, 2 * P * mt : 2 * P * (mt + 1)].bitcast(FP4X4),
                lhsT_scale=w_plane[:, s, P * mt : P * (mt + 1)],
                rhs=codes[:, col : col + BLOCK].bitcast(FP8X4),
                rhs_scale=plane[:, col : col + BLOCK],
                start=(s == 0), stop=(s == STATS - 1),
            )

        out_tiles = out.rearrange("(mt p) v -> p mt v", p=P)

        moving = [quantise("mean0", mean[0][:], HALF)]
        ends = extremes(pair_up(0), 0, 0, HALF)
        moving.extend(quantise("ends0_%d" % s, ends[s][:], HALF) for s in range(2))
        acc = bank(4, "out_acc", [P, N // P, HALF])
        for b in range(HALF // BLOCK):
            for mt in range(N // P):
                for s in range(STATS):
                    product(acc[:, mt, BLOCK * b : BLOCK * (b + 1)], mt, s, moving[s], BLOCK * b)
        result = sb("result0", [P, N // P, HALF], F32)
        nc.scalar.copy(out=result[:], in_=acc[:])
        nc.sync.dma_start(out=out_tiles[:, :, 0:HALF], in_=result[:])

        second = pair_up(HALF)
        for v0 in (HALF, HALF + BLOCK):
            last = v0 + BLOCK == T
            ends = extremes(second, HALF, v0, BLOCK)
            if not last:
                means = quantise("mean%d" % HALF, mean[HALF][:], HALF)
            moving = [(means, v0 - HALF)]
            moving.extend((quantise("ends%d_%d" % (v0, s), ends[s][:], BLOCK), 0) for s in range(2))
            accs = [bank((0 if last else 6) + mt, "out_acc%d_%d" % (v0, mt), [P, BLOCK]) for mt in range(N // P)]
            for s in range(STATS):
                for mt in range(N // P):
                    product(accs[mt][:], mt, s, *moving[s])
            for mt in range(N // P):
                result = sb("result%d_%d" % (v0, mt), [P, BLOCK], F32)
                if last and mt == 0:
                    nc.vector.tensor_copy(out=result[:], in_=accs[mt][:])
                else:
                    nc.scalar.copy(out=result[:], in_=accs[mt][:])
                queue = nc.scalar if last and mt == 1 else nc.sync
                queue.dma_start(out=out_tiles[:, mt, v0 : v0 + BLOCK], in_=result[:])
